import numpy as np
CORES = [2,10,18,26,34,42,50,58,66,74,82,90,98,106,114,122,130,138,146,154,162,170,178,186,194,202,210,218,226,234,242,250]
N = 32
def setup_inputs(rng):
    return {"x": rng.standard_normal((N, 128, 32), dtype=np.float32)}
def reference(x):
    b = 32 // N
    blocks = x.reshape(N, 128, N, b)
    return {"y": np.ascontiguousarray(blocks.transpose(2, 1, 0, 3)).reshape(N, 128, 32)}

@@ -1,0 +1,24 @@
+SCRATCH = {
+    "xs": ("sbuf", [128, 32], "float32"),
+    "land": ("sbuf", [128, 32], "float32"),
+}
+SEMAPHORES = ["loaded", "read", "arrived", "stored"]
+
+
+def rank_program(g, core, T, topo):
+    r = T.rank_of(core)
+    if r is None:
+        return
+    n = len(T.cores)
+    g.dma_start(T.xs[:], T.x[:]).then_inc(T.sem.loaded, 16)
+    g.wait_ge(T.sem.loaded, 16)
+    for k in range(1, n):
+        j = (r + k) % n
+        rid, pid = topo.addr(T.cores[j], core)
+        g.remote_dma(T.land[:, r:r + 1], T.xs[:, j:j + 1], T.sem.arrived, T.sem.read, pid, rid, 0xFF)
+    g.dma_start(T.land[:, r:r + 1], T.xs[:, r:r + 1]).then_inc(T.sem.loaded, 16)
+    g.wait_ge(T.sem.loaded, 32)
+    g.wait_ge(T.sem.arrived, 8 * (n - 1))
+    g.dma_start(T.y[:], T.land[:]).then_inc(T.sem.stored, 16)
+    g.wait_ge(T.sem.read, 8 * (n - 1))
+    g.wait_ge(T.sem.stored, 16)

@@ -1,3 +1,5 @@
+from concourse.bass import DstId, RemoteDMATransfer
+
 SCRATCH = {
     "xs": ("sbuf", [128, 32], "float32"),
     "land": ("sbuf", [128, 32], "float32"),
@@ -12,13 +14,17 @@ def rank_program(g, core, T, topo):
     n = len(T.cores)
     g.dma_start(T.xs[:], T.x[:]).then_inc(T.sem.loaded, 16)
     g.wait_ge(T.sem.loaded, 16)
-    for k in range(1, n):
-        j = (r + k) % n
-        rid, pid = topo.addr(T.cores[j], core)
-        g.remote_dma(T.land[:, r:r + 1], T.xs[:, j:j + 1], T.sem.arrived, T.sem.read, pid, rid, 0xFF)
+    order = [(r + k) % n for k in range(1, n)]
+    for c0 in range(0, len(order), 8):
+        trs = []
+        for e, j in enumerate(order[c0:c0 + 8]):
+            rid, pid = topo.addr(T.cores[j], core)
+            trs.append(RemoteDMATransfer(dst_ids=[DstId(rid=rid, pnc=pid)], dma_engine_mask=1 << e,
+                                         remote_sem=T.sem.arrived, src=T.xs[:, j:j + 1], dst=T.land[:, r:r + 1]))
+        g.remote_dma_fused(trs, local_sem=T.sem.read)
     g.dma_start(T.land[:, r:r + 1], T.xs[:, r:r + 1]).then_inc(T.sem.loaded, 16)
     g.wait_ge(T.sem.loaded, 32)
-    g.wait_ge(T.sem.arrived, 8 * (n - 1))
+    g.wait_ge(T.sem.arrived, n - 1)
     g.dma_start(T.y[:], T.land[:]).then_inc(T.sem.stored, 16)
-    g.wait_ge(T.sem.read, 8 * (n - 1))
+    g.wait_ge(T.sem.read, n - 1)
     g.wait_ge(T.sem.stored, 16)

@@ -4,27 +4,48 @@ SCRATCH = {
     "xs": ("sbuf", [128, 32], "float32"),
     "land": ("sbuf", [128, 32], "float32"),
 }
-SEMAPHORES = ["loaded", "read", "arrived", "stored"]
+SEMAPHORES = ["loaded", "given", "read", "arrived", "stored"]
+
+PAIRS = ((0, 2), (1, 3), (4, 6), (5, 7))
 
 
 def rank_program(g, core, T, topo):
-    r = T.rank_of(core)
-    if r is None:
-        return
+    base = core - core % 8
+    owner = base + 2
+    r = T.rank_of(owner)
     n = len(T.cores)
-    g.dma_start(T.xs[:], T.x[:]).then_inc(T.sem.loaded, 16)
-    g.wait_ge(T.sem.loaded, 16)
-    order = [(r + k) % n for k in range(1, n)]
-    for c0 in range(0, len(order), 8):
+    me = core % 8
+    k = [me in p for p in PAIRS].index(True)
+    other_parity = PAIRS[k][1] == me
+
+    if core == owner:
+        g.dma_start(T.xs[:], T.x[:]).then_inc(T.sem.loaded, 16)
+        g.wait_ge(T.sem.loaded, 16)
         trs = []
-        for e, j in enumerate(order[c0:c0 + 8]):
-            rid, pid = topo.addr(T.cores[j], core)
-            trs.append(RemoteDMATransfer(dst_ids=[DstId(rid=rid, pnc=pid)], dma_engine_mask=1 << e,
-                                         remote_sem=T.sem.arrived, src=T.xs[:, j:j + 1], dst=T.land[:, r:r + 1]))
+        for q, pair in enumerate(PAIRS):
+            dsts = [base + c for c in pair if base + c != core]
+            ids = [topo.addr(d, core) for d in dsts]
+            trs.append(RemoteDMATransfer(dst_ids=[DstId(rid=a[0], pnc=a[1]) for a in ids],
+                                         dma_engine_mask=0xF << (4 * q), remote_sem=T.sem.given,
+                                         srcs=[T.xs[:, 8 * q:8 * q + 8]],
+                                         dsts=[T.xs[:, 8 * q:8 * q + 8] for d in dsts]))
         g.remote_dma_fused(trs, local_sem=T.sem.read)
-    g.dma_start(T.land[:, r:r + 1], T.xs[:, r:r + 1]).then_inc(T.sem.loaded, 16)
-    g.wait_ge(T.sem.loaded, 32)
-    g.wait_ge(T.sem.arrived, n - 1)
-    g.dma_start(T.y[:], T.land[:]).then_inc(T.sem.stored, 16)
-    g.wait_ge(T.sem.read, n - 1)
-    g.wait_ge(T.sem.stored, 16)
+    else:
+        g.wait_ge(T.sem.given, 4)
+
+    want = (r + 1) % 2 if other_parity else r % 2
+    cols = [j for j in range(8 * k, 8 * k + 8) if j % 2 == want]
+    trs = []
+    for e, j in enumerate(cols):
+        rid, pid = topo.addr(T.cores[j], core)
+        trs.append(RemoteDMATransfer(dst_ids=[DstId(rid=rid, pnc=pid)], dma_engine_mask=0x3 << (2 * e),
+                                     remote_sem=T.sem.arrived, src=T.xs[:, j:j + 1], dst=T.land[:, r:r + 1]))
+    g.remote_dma_fused(trs, local_sem=T.sem.read)
+
+    if core == owner:
+        g.wait_ge(T.sem.arrived, 2 * n)
+        g.dma_start(T.y[:], T.land[:]).then_inc(T.sem.stored, 16)
+        g.wait_ge(T.sem.read, 16 + 8)
+        g.wait_ge(T.sem.stored, 16)
+    else:
+        g.wait_ge(T.sem.read, 8)

@@ -6,46 +6,53 @@ SCRATCH = {
 }
 SEMAPHORES = ["loaded", "given", "read", "arrived", "stored"]
 
-PAIRS = ((0, 2), (1, 3), (4, 6), (5, 7))
+OWN = (2, 3, 0, 1)
+GUEST = (6, 7, 4, 5)
+
+
+def own_group(r, i):
+    return (r // 8 + 1 + i) % 4
 
 
 def rank_program(g, core, T, topo):
     base = core - core % 8
-    owner = base + 2
-    r = T.rank_of(owner)
-    n = len(T.cores)
     me = core % 8
-    k = [me in p for p in PAIRS].index(True)
-    other_parity = PAIRS[k][1] == me
+    home = T.rank_of(base + 2)
+    n = len(T.cores)
+    is_rank = me == 2
 
-    if core == owner:
+    if is_rank:
         g.dma_start(T.xs[:], T.x[:]).then_inc(T.sem.loaded, 16)
         g.wait_ge(T.sem.loaded, 16)
+        mate_base = T.cores[home ^ 1] - 2
+        plan = [(mate_base + c, i, 2 * i) for i, c in enumerate(GUEST)]
+        plan += [(base + OWN[i], own_group(home, i), 8 + 2 * (i - 1)) for i in (1, 2, 3)]
         trs = []
-        for q, pair in enumerate(PAIRS):
-            dsts = [base + c for c in pair if base + c != core]
-            ids = [topo.addr(d, core) for d in dsts]
-            trs.append(RemoteDMATransfer(dst_ids=[DstId(rid=a[0], pnc=a[1]) for a in ids],
-                                         dma_engine_mask=0xF << (4 * q), remote_sem=T.sem.given,
-                                         srcs=[T.xs[:, 8 * q:8 * q + 8]],
-                                         dsts=[T.xs[:, 8 * q:8 * q + 8] for d in dsts]))
+        for d, k, e in plan:
+            rid, pid = topo.addr(d, core)
+            trs.append(RemoteDMATransfer(dst_ids=[DstId(rid=rid, pnc=pid)], dma_engine_mask=0x3 << e,
+                                         remote_sem=T.sem.given, src=T.xs[:, 8 * k:8 * k + 8],
+                                         dst=T.xs[:, 8 * k:8 * k + 8]))
         g.remote_dma_fused(trs, local_sem=T.sem.read)
     else:
-        g.wait_ge(T.sem.given, 4)
+        g.wait_ge(T.sem.given, 2)
 
-    want = (r + 1) % 2 if other_parity else r % 2
-    cols = [j for j in range(8 * k, 8 * k + 8) if j % 2 == want]
+    if me in OWN:
+        s, k = home, own_group(home, OWN.index(me))
+    else:
+        s, k = home ^ 1, GUEST.index(me)
+    cols = [j for j in range(8 * k, 8 * k + 8) if j % 2 == home % 2]
     trs = []
     for e, j in enumerate(cols):
         rid, pid = topo.addr(T.cores[j], core)
         trs.append(RemoteDMATransfer(dst_ids=[DstId(rid=rid, pnc=pid)], dma_engine_mask=0x3 << (2 * e),
-                                     remote_sem=T.sem.arrived, src=T.xs[:, j:j + 1], dst=T.land[:, r:r + 1]))
+                                     remote_sem=T.sem.arrived, src=T.xs[:, j:j + 1], dst=T.land[:, s:s + 1]))
     g.remote_dma_fused(trs, local_sem=T.sem.read)
 
-    if core == owner:
+    if is_rank:
         g.wait_ge(T.sem.arrived, 2 * n)
         g.dma_start(T.y[:], T.land[:]).then_inc(T.sem.stored, 16)
-        g.wait_ge(T.sem.read, 16 + 8)
+        g.wait_ge(T.sem.read, 14 + 8)
         g.wait_ge(T.sem.stored, 16)
     else:
         g.wait_ge(T.sem.read, 8)

from concourse.bass import DstId, RemoteDMATransfer

SCRATCH = {
    "xs": ("sbuf", [128, 32], "float32"),
    "land": ("sbuf", [128, 32], "float32"),
}
SEMAPHORES = ["loaded", "given", "read", "arrived", "stored"]

OWN = (2, 3, 0, 1)
GUEST = (6, 7, 4, 5)


def own_group(r, i):
    return (r // 8 + 1 + i) % 4


def rank_program(g, core, T, topo):
    base = core - core % 8
    me = core % 8
    home = T.rank_of(base + 2)
    n = len(T.cores)
    is_rank = me == 2

    if is_rank:
        g.dma_start(T.xs[:], T.x[:]).then_inc(T.sem.loaded, 16)
        g.wait_ge(T.sem.loaded, 16)
        mate_base = T.cores[home ^ 1] - 2
        plan = [(mate_base + c, i, 2 * i) for i, c in enumerate(GUEST)]
        plan += [(base + OWN[i], own_group(home, i), 8 + 2 * (i - 1)) for i in (1, 2, 3)]
        trs = []
        for d, k, e in plan:
            rid, pid = topo.addr(d, core)
            trs.append(RemoteDMATransfer(dst_ids=[DstId(rid=rid, pnc=pid)], dma_engine_mask=0x3 << e,
                                         remote_sem=T.sem.given, src=T.xs[:, 8 * k:8 * k + 8],
                                         dst=T.xs[:, 8 * k:8 * k + 8]))
        g.remote_dma_fused(trs, local_sem=T.sem.read)
    else:
        g.wait_ge(T.sem.given, 2)

    if me in OWN:
        s, k = home, own_group(home, OWN.index(me))
    else:
        s, k = home ^ 1, GUEST.index(me)
    cols = [j for j in range(8 * k, 8 * k + 8) if j % 2 == home % 2]
    trs = []
    for e, j in enumerate(cols):
        rid, pid = topo.addr(T.cores[j], core)
        trs.append(RemoteDMATransfer(dst_ids=[DstId(rid=rid, pnc=pid)], dma_engine_mask=0x3 << (2 * e),
                                     remote_sem=T.sem.arrived, src=T.xs[:, j:j + 1], dst=T.land[:, s:s + 1]))
    g.remote_dma_fused(trs, local_sem=T.sem.read)

    if is_rank:
        g.wait_ge(T.sem.arrived, 2 * n)
        g.dma_start(T.y[:], T.land[:]).then_inc(T.sem.stored, 16)
        g.wait_ge(T.sem.read, 14 + 8)
        g.wait_ge(T.sem.stored, 16)
    else:
        g.wait_ge(T.sem.read, 8)
